import numpy as np
import ml_dtypes


def mxq(x, axis, fmt="e4m3"):
    dtype, down = {"e4m3": (ml_dtypes.float8_e4m3fn, 7), "e5m2": (ml_dtypes.float8_e5m2, 14)}[fmt]
    v = np.moveaxis(np.asarray(x, np.float32).astype(ml_dtypes.bfloat16).astype(np.float64), axis, -1)
    blocks = v.reshape(v.shape[:-1] + (-1, 32))
    amax = np.abs(blocks).max(-1, keepdims=True)
    byte = np.maximum(np.where(amax > 0, np.frexp(amax)[1] - 1 + 127, 0) - down, 1)
    scale = np.exp2(byte - 127.0)
    codes = (blocks / scale).astype(np.float32).astype(dtype).astype(np.float64)
    return np.moveaxis((codes * scale).reshape(v.shape), -1, axis)


WIDE = False


def mx_kscale(k):
    if not WIDE:
        return np.ones(k)
    levels = np.array([10, -10, 5, -5, 0])
    if k % 512:
        return np.exp2(np.random.permutation(np.resize(levels, k // 32))).repeat(32)
    a = np.empty((k // 512, 16))
    for p in range(k // 512):
        a[p, :8] = np.random.permutation(np.resize(levels, 8))
        for g in range(8):
            far = levels[np.abs(levels - a[p, g]) >= 10]
            a[p, g + 8] = far[np.random.randint(len(far))]
    return np.exp2(a.ravel()).repeat(32)


def f64(x):
    return np.asarray(x).astype(np.float64)


def striped8(idx):
    return np.asarray(idx).reshape(8, -1, 16).transpose(0, 2, 1).reshape(128, -1).astype(np.uint16)


def unstriped8(offs):
    return offs.reshape(8, 16, -1).transpose(0, 2, 1).reshape(8, -1).astype(np.int64)


def pick8(x, idx, run):
    r = np.arange(len(x))
    return x[r[:, None], idx[r % (8 * run) // run]]


E2M1 = np.array([0.0, 0.5, 1.0, 1.5, 2.0, 3.0, 4.0, 6.0, -0.0, -0.5, -1.0, -1.5, -2.0, -3.0, -4.0, -6.0])


def pack_weight(w, fmt):
    k, n = w.shape
    w = f64(np.asarray(w, np.float32).astype(ml_dtypes.bfloat16)).reshape(k // 32, 32, n)
    amax = np.abs(w).max(1)
    if fmt == "e4m3":
        byte = np.frexp(amax)[1] - 1 + 127 - 7
    else:
        mant, ex = np.frexp(amax / 6.0)
        byte = np.where(mant > 0.5, ex, ex - 1) + 127
    byte = np.clip(np.where(amax > 0, byte, 1), 1, 254)
    scaled = (w * np.exp2(127.0 - byte)[:, None, :]).reshape(k, n).astype(np.float32)
    by_word = np.ascontiguousarray(scaled.reshape(k // 512, 128, 4, n).transpose(0, 1, 3, 2))
    if fmt == "e4m3":
        words = by_word.astype(ml_dtypes.float8_e4m3fn).view(np.uint8)
    else:
        c = by_word.astype(ml_dtypes.float4_e2m1fn).view(np.uint8) & 0xF
        words = (c[..., 0::2] | (c[..., 1::2] << 4)).reshape(k // 512, 128, 2 * n)
    return np.ascontiguousarray(words), np.ascontiguousarray(byte.astype(np.uint8).reshape(k // 512, 16, n))


def unpack_weight(words, scales, fmt):
    g, _, n = scales.shape
    words = np.ascontiguousarray(words).reshape(g, 128, n, -1)
    if fmt == "e4m3":
        vals = words.view(ml_dtypes.float8_e4m3fn).astype(np.float64)
    else:
        nib = np.empty((g, 128, n, 4), np.uint8)
        nib[..., 0::2] = words & 0xF
        nib[..., 1::2] = words >> 4
        vals = E2M1[nib]
    vals = vals * np.repeat(np.exp2(scales.astype(np.float64) - 127.0), 8, axis=1)[..., None]
    return vals.transpose(0, 1, 3, 2).reshape(g * 512, n)


D, T, I, Q = 512, 1024, 512, 128


def setup_inputs():
    n = np.random.standard_normal
    idx = np.stack([np.random.permutation(T)[:I] for _ in range(8)])
    idx2 = np.stack([np.random.permutation(T)[:I] for _ in range(8)])
    idx3 = np.stack([np.random.permutation(T)[:I] for _ in range(8)])
    idx4 = np.stack([np.random.permutation(T)[:I] for _ in range(8)])
    fd = mx_kscale(D)
    keysp = pack_weight(n((D, T)) / fd[:, None], "e4m3")
    return {
        "query": (n((D, Q)) * 0.9 / np.sqrt(D) * fd[:, None]).astype(np.float32),
        "query2": (n((D, Q)) * 0.9 / np.sqrt(D) * fd[:, None]).astype(np.float32),
        "keys_words": keysp[0],
        "keys_scales": keysp[1],
        "lam": (np.random.uniform(1.0, 2.5, (Q, 1))).astype(np.float32),
        "old": (1.0 * n((Q, T))).astype(np.float32),
        "share2": (np.random.uniform(0.4, 1.2, (Q, 1))).astype(np.float32),
        "offs": striped8(idx),
        "offs2": striped8(idx2),
        "offs3": striped8(idx3),
        "offs4": striped8(idx4),
    }


def reference(query, query2, keys_words, keys_scales, lam, old, share2, offs, offs2, offs3, offs4):
    idx = unstriped8(offs)
    idx2 = unstriped8(offs2)
    idx3 = unstriped8(offs3)
    idx4 = unstriped8(offs4)
    keysu = unpack_weight(keys_words, keys_scales, "e4m3")
    queryq = mxq(f64(query), 0, "e4m3")
    a = queryq.T @ keysu
    query2q = mxq(f64(query2), 0, "e4m3")
    b = query2q.T @ keysu
    e1s = np.exp(pick8(a, idx, 16))
    w = e1s / (e1s + np.exp(pick8(a, idx2, 16)) + np.exp(pick8(b, idx3, 16))) * f64(lam)
    f1 = np.zeros((Q, T))
    f1[np.arange(Q)[:, None], idx[np.arange(Q) % 128 // 16]] = w
    f2 = np.zeros((Q, T))
    f2[np.arange(Q)[:, None], idx4[np.arange(Q) % 128 // 16]] = w
    y = f64(old) + f1 + f2 * f64(share2)
    return y

@@ -1,0 +1,168 @@
+from contextlib import ExitStack
+
+import concourse.mybir as mybir
+from concourse.masks import make_identity
+
+D, T, I, Q = 512, 1024, 512, 128
+FLOPS = 2 * 2 * D * T * Q
+
+F32 = mybir.dt.float32
+BF16 = mybir.dt.bfloat16
+I32 = mybir.dt.int32
+U32 = mybir.dt.uint32
+U16 = mybir.dt.uint16
+U8 = mybir.dt.uint8
+FP8X4 = mybir.dt.float8_e4m3fn_x4
+ALU = mybir.AluOpType
+ACT = mybir.ActivationFunctionType
+
+P = 128
+PACK = 4
+BANK = 512
+GROUP = 16
+HALF = I // 2
+FIRST = 128
+STORES = 4
+
+
+def tile_attend_quotaratio_lean_twiceput_heads_kernel(
+    tc, query, query2, keys_words, keys_scales, lam, old, share2, offs, offs2, offs3, offs4, out
+):
+    nc = tc.nc
+    with ExitStack() as ctx:
+        sb = ctx.enter_context(tc.tile_pool(name="sb", bufs=1))
+        ps = ctx.enter_context(tc.psum_pool(name="ps", bufs=1))
+
+        def entries(list_tile, lo, hi):
+            return list_tile[:, lo // GROUP : hi // GROUP]
+
+        key_scales = sb.tile([P, T], U8, name="key_scales", align_bytes=64)
+        nc.vector.memset(key_scales[:].bitcast(I32), 0)
+
+        raw = []
+        for n, src in enumerate((query, query2)):
+            t = sb.tile([P, PACK, Q], F32, name="raw%d" % n)
+            nc.sync.dma_start(out=t[:], in_=src.rearrange("(p j) q -> p j q", j=PACK))
+            raw.append(t)
+        words_hbm = keys_words[0].rearrange("p n t -> p (n t)").bitcast(I32)
+        key_words = []
+        for h in range(T // BANK):
+            t = sb.tile([P, BANK], U32, name="key_words%d" % h, align_bytes=64)
+            nc.sync.dma_start(out=t[:].bitcast(I32), in_=words_hbm[:, h * BANK : (h + 1) * BANK])
+            key_words.append(t)
+        scales_hbm = keys_scales[0].bitcast(I32)
+        for quad in range(4):
+            nc.scalar.dma_start(
+                out=key_scales[32 * quad : 32 * quad + 4, :].bitcast(I32),
+                in_=scales_hbm[4 * quad : 4 * quad + 4, :],
+            )
+        lists = []
+        for n, src in enumerate((offs, offs2, offs3, offs4)):
+            t = sb.tile([P, I // GROUP], U16, name="list%d" % n)
+            nc.sync.dma_start(t[:], src)
+            lists.append(t)
+        list1, list2, list3, list4 = lists
+        lam_sb = sb.tile([P, 1], F32, name="lam_sb")
+        nc.gpsimd.dma_start(out=lam_sb[:], in_=lam)
+        share_sb = sb.tile([P, 1], F32, name="share_sb")
+        nc.gpsimd.dma_start(out=share_sb[:], in_=share2)
+        old_sb = sb.tile([P, T], F32, name="old_sb")
+        nc.sync.dma_start(out=old_sb[:], in_=old)
+
+        ident = sb.tile([P, P], F32, name="ident")
+        make_identity(nc, ident[:])
+        f1 = sb.tile([P, T], F32, name="f1")
+        f2 = sb.tile([P, T], F32, name="f2")
+        nc.vector.memset(f1[:], 0.0)
+        nc.vector.memset(f2[:], 0.0)
+
+        banks = []
+        for n in range(2):
+            grouped = sb.tile([P, Q, PACK], BF16, name="grouped%d" % n, align_bytes=64)
+            nc.vector.tensor_copy(
+                out=grouped[:].rearrange("p (c i) t -> p c t i", i=4),
+                in_=raw[n][:].rearrange("p t (c i) -> p c t i", i=4),
+            )
+            codes = sb.tile([P, Q], U32, name="codes%d" % n, align_bytes=64)
+            scales = sb.tile([P, Q], U8, name="scales%d" % n, align_bytes=64)
+            nc.vector.quantize_mx(
+                out=codes[:].bitcast(FP8X4), scales=scales[:], in_=grouped[:].rearrange("p q t -> p (q t)")
+            )
+            for h in range(T // BANK):
+                bank = ps.tile([P, BANK], F32, name="score%d_%d" % (n, h))
+                nc.tensor.matmul_mx(
+                    out=bank[:],
+                    lhsT=codes[:].bitcast(FP8X4),
+                    lhsT_scale=scales[:],
+                    rhs=key_words[h][:].bitcast(FP8X4),
+                    rhs_scale=key_scales[:, h * BANK : (h + 1) * BANK],
+                    start=True,
+                    stop=True,
+                )
+                banks.append(bank)
+
+        a = sb.tile([P, T], F32, name="a")
+        b = sb.tile([P, T], F32, name="b")
+        nc.scalar.copy(out=a[:, :BANK], in_=banks[0][:])
+        nc.vector.tensor_copy(out=a[:, BANK:], in_=banks[1][:])
+        a1 = sb.tile([P, I], F32, name="a1")
+        nc.vector.tensor_copy(out=a1[:, :HALF], in_=a[:].indirect(entries(list1, 0, HALF)))
+        nc.scalar.activation(a1[:, HALF:], a[:].indirect(entries(list1, HALF, I)), ACT.Copy)
+        nc.scalar.copy(out=b[:, :BANK], in_=banks[2][:])
+        nc.scalar.copy(out=b[:, BANK:], in_=banks[3][:])
+
+        d2 = sb.tile([P, I], F32, name="d2")
+        nc.vector.tensor_tensor(d2[:], a[:].indirect(list2[:]), a1[:], ALU.subtract)
+        u = sb.tile([P, I], F32, name="u")
+        nc.scalar.activation(u[:], d2[:], ACT.Exp)
+        d3 = sb.tile([P, I], F32, name="d3")
+        v = sb.tile([P, I], F32, name="v")
+        s = sb.tile([P, I], F32, name="s")
+        for lo in (0, HALF):
+            nc.vector.tensor_tensor(
+                d3[:, lo : lo + HALF], b[:].indirect(entries(list3, lo, lo + HALF)), a1[:, lo : lo + HALF], ALU.subtract
+            )
+            nc.scalar.activation(v[:, lo : lo + HALF], d3[:, lo : lo + HALF], ACT.Exp)
+        for lo in (0, HALF):
+            nc.vector.tensor_tensor(s[:, lo : lo + HALF], u[:, lo : lo + HALF], v[:, lo : lo + HALF], ALU.add)
+
+        turned = []
+        for h in range(T // BANK):
+            bank = ps.tile([P, BANK], F32, name="turned%d" % h)
+            for j in range(BANK // P):
+                c = h * BANK + j * P
+                nc.tensor.matmul(bank[:, j * P : (j + 1) * P], lhsT=old_sb[:, c : c + P], rhs=ident[:],
+                                 start=(j == 0), stop=False, is_transpose=True)
+            turned.append(bank)
+
+        root = sb.tile([P, I], F32, name="root")
+        root_lam = sb.tile([P, I], F32, name="root_lam")
+        for lo, hi in ((0, FIRST), (FIRST, I)):
+            nc.scalar.activation(root[:, lo:hi], s[:, lo:hi], ACT.Abs_reciprocal_sqrt, bias=1.0)
+            nc.scalar.activation(root_lam[:, lo:hi], root[:, lo:hi], ACT.Copy, scale=lam_sb[:])
+            nc.vector.tensor_tensor(f1[:].indirect(entries(list1, lo, hi)), root[:, lo:hi], root_lam[:, lo:hi], ALU.mult)
+        nc.vector.tensor_tensor(f2[:].indirect(list4[:]), root[:], root_lam[:], ALU.mult)
+
+        result = sb.tile([P, T], F32, name="result")
+        width = T // STORES
+        for h in range(T // BANK):
+            for j in range(BANK // P):
+                c = h * BANK + j * P
+                nc.tensor.matmul(turned[h][:, j * P : (j + 1) * P], lhsT=f1[:, c : c + P], rhs=ident[:],
+                                 start=False, stop=(j == BANK // P - 1), is_transpose=True)
+        backs = []
+        for h in range(T // BANK):
+            staged = sb.tile([P, BANK], F32, name="staged%d" % h)
+            nc.scalar.copy(out=staged[:], in_=turned[h][:])
+            back = ps.tile([P, BANK], F32, name="back%d" % h)
+            for j in range(BANK // P):
+                nc.tensor.transpose(back[:, j * P : (j + 1) * P], staged[:, j * P : (j + 1) * P], ident[:])
+            backs.append(back)
+        for k in range(STORES):
+            c = k * width
+            nc.vector.scalar_tensor_tensor(
+                result[:, c : c + width], f2[:, c : c + width], share_sb[:],
+                backs[c // BANK][:, c % BANK : c % BANK + width], ALU.mult, ALU.add,
+            )
+            queue = nc.sync if k % 2 == 0 else nc.scalar
+            queue.dma_start(out=out[:, c : c + width], in_=result[:, c : c + width])

@@ -37,25 +37,23 @@ def tile_attend_quotaratio_lean_twiceput_heads_kernel(
             return list_tile[:, lo // GROUP : hi // GROUP]
 
         key_scales = sb.tile([P, T], U8, name="key_scales", align_bytes=64)
-        nc.vector.memset(key_scales[:].bitcast(I32), 0)
+        nc.gpsimd.memset(key_scales[:].bitcast(I32), 0)
 
-        raw = []
-        for n, src in enumerate((query, query2)):
-            t = sb.tile([P, PACK, Q], F32, name="raw%d" % n)
-            nc.sync.dma_start(out=t[:], in_=src.rearrange("(p j) q -> p j q", j=PACK))
-            raw.append(t)
+        raw = [sb.tile([P, PACK, Q], F32, name="raw%d" % n) for n in range(2)]
+        nc.sync.dma_start(out=raw[0][:], in_=query.rearrange("(p j) q -> p j q", j=PACK))
+        scales_hbm = keys_scales[0].bitcast(I32)
+        for quad in range(4):
+            nc.sync.dma_start(
+                out=key_scales[32 * quad : 32 * quad + 4, :].bitcast(I32),
+                in_=scales_hbm[4 * quad : 4 * quad + 4, :],
+            )
+        nc.sync.dma_start(out=raw[1][:], in_=query2.rearrange("(p j) q -> p j q", j=PACK))
         words_hbm = keys_words[0].rearrange("p n t -> p (n t)").bitcast(I32)
         key_words = []
         for h in range(T // BANK):
             t = sb.tile([P, BANK], U32, name="key_words%d" % h, align_bytes=64)
             nc.sync.dma_start(out=t[:].bitcast(I32), in_=words_hbm[:, h * BANK : (h + 1) * BANK])
             key_words.append(t)
-        scales_hbm = keys_scales[0].bitcast(I32)
-        for quad in range(4):
-            nc.scalar.dma_start(
-                out=key_scales[32 * quad : 32 * quad + 4, :].bitcast(I32),
-                in_=scales_hbm[4 * quad : 4 * quad + 4, :],
-            )
         lists = []
         for n, src in enumerate((offs, offs2, offs3, offs4)):
             t = sb.tile([P, I // GROUP], U16, name="list%d" % n)
@@ -63,9 +61,9 @@ def tile_attend_quotaratio_lean_twiceput_heads_kernel(
             lists.append(t)
         list1, list2, list3, list4 = lists
         lam_sb = sb.tile([P, 1], F32, name="lam_sb")
-        nc.gpsimd.dma_start(out=lam_sb[:], in_=lam)
+        nc.sync.dma_start(out=lam_sb[:], in_=lam)
         share_sb = sb.tile([P, 1], F32, name="share_sb")
-        nc.gpsimd.dma_start(out=share_sb[:], in_=share2)
+        nc.sync.dma_start(out=share_sb[:], in_=share2)
         old_sb = sb.tile([P, T], F32, name="old_sb")
         nc.sync.dma_start(out=old_sb[:], in_=old)
 
@@ -89,7 +87,7 @@ def tile_attend_quotaratio_lean_twiceput_heads_kernel(
                 out=codes[:].bitcast(FP8X4), scales=scales[:], in_=grouped[:].rearrange("p q t -> p (q t)")
             )
             for h in range(T // BANK):
-                bank = ps.tile([P, BANK], F32, name="score%d_%d" % (n, h))
+                bank = ps.tile([P, BANK], F32, name="score%d" % len(banks), tag="score%d" % len(banks))
                 nc.tensor.matmul_mx(
                     out=bank[:],
                     lhsT=codes[:].bitcast(FP8X4),
@@ -105,64 +103,75 @@ def tile_attend_quotaratio_lean_twiceput_heads_kernel(
         b = sb.tile([P, T], F32, name="b")
         nc.scalar.copy(out=a[:, :BANK], in_=banks[0][:])
         nc.vector.tensor_copy(out=a[:, BANK:], in_=banks[1][:])
+        nc.scalar.copy(out=b[:, :BANK], in_=banks[2][:])
+        nc.scalar.copy(out=b[:, BANK:], in_=banks[3][:])
         a1 = sb.tile([P, I], F32, name="a1")
         nc.vector.tensor_copy(out=a1[:, :HALF], in_=a[:].indirect(entries(list1, 0, HALF)))
         nc.scalar.activation(a1[:, HALF:], a[:].indirect(entries(list1, HALF, I)), ACT.Copy)
-        nc.scalar.copy(out=b[:, :BANK], in_=banks[2][:])
-        nc.scalar.copy(out=b[:, BANK:], in_=banks[3][:])
 
         d2 = sb.tile([P, I], F32, name="d2")
-        nc.vector.tensor_tensor(d2[:], a[:].indirect(list2[:]), a1[:], ALU.subtract)
-        u = sb.tile([P, I], F32, name="u")
-        nc.scalar.activation(u[:], d2[:], ACT.Exp)
         d3 = sb.tile([P, I], F32, name="d3")
+        u = sb.tile([P, I], F32, name="u")
         v = sb.tile([P, I], F32, name="v")
         s = sb.tile([P, I], F32, name="s")
-        for lo in (0, HALF):
-            nc.vector.tensor_tensor(
-                d3[:, lo : lo + HALF], b[:].indirect(entries(list3, lo, lo + HALF)), a1[:, lo : lo + HALF], ALU.subtract
-            )
-            nc.scalar.activation(v[:, lo : lo + HALF], d3[:, lo : lo + HALF], ACT.Exp)
-        for lo in (0, HALF):
-            nc.vector.tensor_tensor(s[:, lo : lo + HALF], u[:, lo : lo + HALF], v[:, lo : lo + HALF], ALU.add)
 
-        turned = []
-        for h in range(T // BANK):
-            bank = ps.tile([P, BANK], F32, name="turned%d" % h)
-            for j in range(BANK // P):
-                c = h * BANK + j * P
-                nc.tensor.matmul(bank[:, j * P : (j + 1) * P], lhsT=old_sb[:, c : c + P], rhs=ident[:],
-                                 start=(j == 0), stop=False, is_transpose=True)
-            turned.append(bank)
+        def ratio(lo, window, list_tile, diff, power):
+            cols = slice(lo, lo + HALF)
+            nc.vector.tensor_tensor(
+                diff[:, cols], window[:].indirect(entries(list_tile, lo, lo + HALF)), a1[:, cols], ALU.subtract
+            )
+            nc.scalar.activation(power[:, cols], diff[:, cols], ACT.Exp)
+
+        def total(lo):
+            cols = slice(lo, lo + HALF)
+            nc.vector.scalar_tensor_tensor(s[:, cols], u[:, cols], 1.0, v[:, cols], ALU.add, ALU.add)
 
         root = sb.tile([P, I], F32, name="root")
         root_lam = sb.tile([P, I], F32, name="root_lam")
-        for lo, hi in ((0, FIRST), (FIRST, I)):
-            nc.scalar.activation(root[:, lo:hi], s[:, lo:hi], ACT.Abs_reciprocal_sqrt, bias=1.0)
-            nc.scalar.activation(root_lam[:, lo:hi], root[:, lo:hi], ACT.Copy, scale=lam_sb[:])
-            nc.vector.tensor_tensor(f1[:].indirect(entries(list1, lo, hi)), root[:, lo:hi], root_lam[:, lo:hi], ALU.mult)
-        nc.vector.tensor_tensor(f2[:].indirect(list4[:]), root[:], root_lam[:], ALU.mult)
 
-        result = sb.tile([P, T], F32, name="result")
+        def put(lo, hi):
+            for window, list_tile in ((f1, list1), (f2, list4)):
+                nc.vector.tensor_tensor(
+                    window[:].indirect(entries(list_tile, lo, hi)), root[:, lo:hi], root_lam[:, lo:hi], ALU.mult
+                )
+
+        nc.gpsimd.tensor_copy(root_lam[:, :FIRST], lam_sb[:].to_broadcast([P, FIRST]))
+        ratio(0, a, list2, d2, u)
+        ratio(0, b, list3, d3, v)
+        ratio(HALF, a, list2, d2, u)
+        total(0)
+        ratio(HALF, b, list3, d3, v)
+        nc.vector.reciprocal(root[:, :FIRST], s[:, :FIRST])
+        total(HALF)
+        put(0, FIRST)
+        nc.scalar.activation(root[:, FIRST:], s[:, FIRST:], ACT.Abs_reciprocal_sqrt)
+        nc.scalar.activation(root_lam[:, FIRST:], root[:, FIRST:], ACT.Copy, scale=lam_sb[:])
+        put(FIRST, I)
+
         width = T // STORES
-        for h in range(T // BANK):
-            for j in range(BANK // P):
-                c = h * BANK + j * P
-                nc.tensor.matmul(turned[h][:, j * P : (j + 1) * P], lhsT=f1[:, c : c + P], rhs=ident[:],
-                                 start=False, stop=(j == BANK // P - 1), is_transpose=True)
-        backs = []
-        for h in range(T // BANK):
-            staged = sb.tile([P, BANK], F32, name="staged%d" % h)
-            nc.scalar.copy(out=staged[:], in_=turned[h][:])
-            back = ps.tile([P, BANK], F32, name="back%d" % h)
-            for j in range(BANK // P):
-                nc.tensor.transpose(back[:, j * P : (j + 1) * P], staged[:, j * P : (j + 1) * P], ident[:])
-            backs.append(back)
+        turned = []
         for k in range(STORES):
+            bank = ps.tile([P, width], F32, name="turned%d" % k)
+            for j in range(width // P):
+                c = k * width + j * P
+                nc.tensor.matmul(bank[:, j * P : (j + 1) * P], lhsT=old_sb[:, c : c + P], rhs=ident[:],
+                                 start=(j == 0), stop=False, is_transpose=True)
+            turned.append(bank)
+        for k in range(STORES):
+            for j in range(width // P):
+                c = k * width + j * P
+                nc.tensor.matmul(turned[k][:, j * P : (j + 1) * P], lhsT=f1[:, c : c + P], rhs=ident[:],
+                                 start=False, stop=(j == width // P - 1), is_transpose=True)
+        result = sb.tile([P, T], F32, name="result")
+        for k in range(STORES):
+            staged = sb.tile([P, width], F32, name="staged%d" % k)
+            nc.scalar.copy(out=staged[:], in_=turned[k][:])
+            back = ps.tile([P, width], F32, name="back%d" % k, tag="score%d" % k)
+            for j in range(width // P):
+                nc.tensor.transpose(back[:, j * P : (j + 1) * P], staged[:, j * P : (j + 1) * P], ident[:])
             c = k * width
             nc.vector.scalar_tensor_tensor(
-                result[:, c : c + width], f2[:, c : c + width], share_sb[:],
-                backs[c // BANK][:, c % BANK : c % BANK + width], ALU.mult, ALU.add,
+                result[:, c : c + width], f2[:, c : c + width], share_sb[:], back[:], ALU.mult, ALU.add
             )
             queue = nc.sync if k % 2 == 0 else nc.scalar
             queue.dma_start(out=out[:, c : c + width], in_=result[:, c : c + width])

@@ -39,7 +39,7 @@ def tile_attend_quotaratio_lean_twiceput_heads_kernel(
         key_scales = sb.tile([P, T], U8, name="key_scales", align_bytes=64)
         nc.gpsimd.memset(key_scales[:].bitcast(I32), 0)
 
-        raw = [sb.tile([P, PACK, Q], F32, name="raw%d" % n) for n in range(2)]
+        raw = [sb.tile([P, PACK, Q], F32, name="raw%d" % n, tag="raw%d" % n) for n in range(2)]
         nc.sync.dma_start(out=raw[0][:], in_=query.rearrange("(p j) q -> p j q", j=PACK))
         scales_hbm = keys_scales[0].bitcast(I32)
         for quad in range(4):
@@ -54,18 +54,16 @@ def tile_attend_quotaratio_lean_twiceput_heads_kernel(
             t = sb.tile([P, BANK], U32, name="key_words%d" % h, align_bytes=64)
             nc.sync.dma_start(out=t[:].bitcast(I32), in_=words_hbm[:, h * BANK : (h + 1) * BANK])
             key_words.append(t)
+        lam_sb = sb.tile([P, 1], F32, name="lam_sb")
+        nc.sync.dma_start(out=lam_sb[:], in_=lam)
         lists = []
         for n, src in enumerate((offs, offs2, offs3, offs4)):
             t = sb.tile([P, I // GROUP], U16, name="list%d" % n)
             nc.sync.dma_start(t[:], src)
             lists.append(t)
         list1, list2, list3, list4 = lists
-        lam_sb = sb.tile([P, 1], F32, name="lam_sb")
-        nc.sync.dma_start(out=lam_sb[:], in_=lam)
         share_sb = sb.tile([P, 1], F32, name="share_sb")
         nc.sync.dma_start(out=share_sb[:], in_=share2)
-        old_sb = sb.tile([P, T], F32, name="old_sb")
-        nc.sync.dma_start(out=old_sb[:], in_=old)
 
         ident = sb.tile([P, P], F32, name="ident")
         make_identity(nc, ident[:])
@@ -74,37 +72,36 @@ def tile_attend_quotaratio_lean_twiceput_heads_kernel(
         nc.vector.memset(f1[:], 0.0)
         nc.vector.memset(f2[:], 0.0)
 
-        banks = []
-        for n in range(2):
+        a = sb.tile([P, T], F32, name="a")
+        b = sb.tile([P, T], F32, name="b")
+        pieces = (
+            ((0, 512, 0, nc.vector.tensor_copy), (512, 768, 1, nc.scalar.copy), (768, 1024, 2, nc.scalar.copy)),
+            ((512, 1024, 3, nc.scalar.copy), (0, 512, 0, nc.scalar.copy)),
+        )
+        for n, scores in enumerate((a, b)):
             grouped = sb.tile([P, Q, PACK], BF16, name="grouped%d" % n, align_bytes=64)
+            codes = sb.tile([P, Q], U32, name="codes%d" % n, align_bytes=64)
+            scales = sb.tile([P, Q], U8, name="scales%d" % n, align_bytes=64)
             nc.vector.tensor_copy(
                 out=grouped[:].rearrange("p (c i) t -> p c t i", i=4),
                 in_=raw[n][:].rearrange("p t (c i) -> p c t i", i=4),
             )
-            codes = sb.tile([P, Q], U32, name="codes%d" % n, align_bytes=64)
-            scales = sb.tile([P, Q], U8, name="scales%d" % n, align_bytes=64)
             nc.vector.quantize_mx(
                 out=codes[:].bitcast(FP8X4), scales=scales[:], in_=grouped[:].rearrange("p q t -> p (q t)")
             )
-            for h in range(T // BANK):
-                bank = ps.tile([P, BANK], F32, name="score%d" % len(banks), tag="score%d" % len(banks))
+            for lo, hi, slot, copy in pieces[n]:
+                bank = ps.tile([P, hi - lo], F32, name="score%d_%d" % (n, lo), tag="bank%d" % slot)
                 nc.tensor.matmul_mx(
                     out=bank[:],
                     lhsT=codes[:].bitcast(FP8X4),
                     lhsT_scale=scales[:],
-                    rhs=key_words[h][:].bitcast(FP8X4),
-                    rhs_scale=key_scales[:, h * BANK : (h + 1) * BANK],
+                    rhs=key_words[lo // BANK][:, lo % BANK : lo % BANK + hi - lo].bitcast(FP8X4),
+                    rhs_scale=key_scales[:, lo:hi],
                     start=True,
                     stop=True,
                 )
-                banks.append(bank)
+                copy(out=scores[:, lo:hi], in_=bank[:])
 
-        a = sb.tile([P, T], F32, name="a")
-        b = sb.tile([P, T], F32, name="b")
-        nc.scalar.copy(out=a[:, :BANK], in_=banks[0][:])
-        nc.vector.tensor_copy(out=a[:, BANK:], in_=banks[1][:])
-        nc.scalar.copy(out=b[:, :BANK], in_=banks[2][:])
-        nc.scalar.copy(out=b[:, BANK:], in_=banks[3][:])
         a1 = sb.tile([P, I], F32, name="a1")
         nc.vector.tensor_copy(out=a1[:, :HALF], in_=a[:].indirect(entries(list1, 0, HALF)))
         nc.scalar.activation(a1[:, HALF:], a[:].indirect(entries(list1, HALF, I)), ACT.Copy)
@@ -135,12 +132,15 @@ def tile_attend_quotaratio_lean_twiceput_heads_kernel(
                     window[:].indirect(entries(list_tile, lo, hi)), root[:, lo:hi], root_lam[:, lo:hi], ALU.mult
                 )
 
-        nc.gpsimd.tensor_copy(root_lam[:, :FIRST], lam_sb[:].to_broadcast([P, FIRST]))
+        nc.scalar.copy(root_lam[:, :FIRST], lam_sb[:].to_broadcast([P, FIRST]))
         ratio(0, a, list2, d2, u)
         ratio(0, b, list3, d3, v)
-        ratio(HALF, a, list2, d2, u)
-        total(0)
+        a2 = sb.tile([P, HALF], F32, name="a2")
+        nc.scalar.activation(a2[:], a[:].indirect(entries(list2, HALF, I)), ACT.Copy)
         ratio(HALF, b, list3, d3, v)
+        total(0)
+        nc.vector.tensor_tensor(d2[:, HALF:], a2[:], a1[:, HALF:], ALU.subtract)
+        nc.scalar.activation(u[:, HALF:], d2[:, HALF:], ACT.Exp)
         nc.vector.reciprocal(root[:, :FIRST], s[:, :FIRST])
         total(HALF)
         put(0, FIRST)
@@ -148,30 +148,27 @@ def tile_attend_quotaratio_lean_twiceput_heads_kernel(
         nc.scalar.activation(root_lam[:, FIRST:], root[:, FIRST:], ACT.Copy, scale=lam_sb[:])
         put(FIRST, I)
 
-        width = T // STORES
+        old_sb = sb.tile([P, T], F32, name="old_sb")
+        nc.sync.dma_start(out=old_sb[:], in_=old)
+        spans = ((0, 256), (256, 512), (512, 896), (896, 1024))
         turned = []
-        for k in range(STORES):
-            bank = ps.tile([P, width], F32, name="turned%d" % k)
-            for j in range(width // P):
-                c = k * width + j * P
-                nc.tensor.matmul(bank[:, j * P : (j + 1) * P], lhsT=old_sb[:, c : c + P], rhs=ident[:],
-                                 start=(j == 0), stop=False, is_transpose=True)
+        for k, (lo, hi) in enumerate(spans):
+            bank = ps.tile([P, hi - lo], F32, name="turned%d" % k, tag="bank%d" % (4 + k))
+            for c in range(lo, hi, P):
+                nc.tensor.matmul(bank[:, c - lo : c - lo + P], lhsT=old_sb[:, c : c + P], rhs=ident[:],
+                                 start=(c == lo), stop=False, is_transpose=True)
             turned.append(bank)
-        for k in range(STORES):
-            for j in range(width // P):
-                c = k * width + j * P
-                nc.tensor.matmul(turned[k][:, j * P : (j + 1) * P], lhsT=f1[:, c : c + P], rhs=ident[:],
-                                 start=False, stop=(j == width // P - 1), is_transpose=True)
+        for k, (lo, hi) in enumerate(spans):
+            for c in range(lo, hi, P):
+                nc.tensor.matmul(turned[k][:, c - lo : c - lo + P], lhsT=f1[:, c : c + P], rhs=ident[:],
+                                 start=False, stop=(c + P == hi), is_transpose=True)
         result = sb.tile([P, T], F32, name="result")
-        for k in range(STORES):
-            staged = sb.tile([P, width], F32, name="staged%d" % k)
+        for k, (lo, hi) in enumerate(spans):
+            staged = sb.tile([P, hi - lo], F32, name="staged%d" % k)
             nc.scalar.copy(out=staged[:], in_=turned[k][:])
-            back = ps.tile([P, width], F32, name="back%d" % k, tag="score%d" % k)
-            for j in range(width // P):
-                nc.tensor.transpose(back[:, j * P : (j + 1) * P], staged[:, j * P : (j + 1) * P], ident[:])
-            c = k * width
-            nc.vector.scalar_tensor_tensor(
-                result[:, c : c + width], f2[:, c : c + width], share_sb[:], back[:], ALU.mult, ALU.add
-            )
+            back = ps.tile([P, hi - lo], F32, name="back%d" % k, tag="bank%d" % k)
+            for c in range(0, hi - lo, P):
+                nc.tensor.transpose(back[:, c : c + P], staged[:, c : c + P], ident[:])
+            nc.vector.scalar_tensor_tensor(result[:, lo:hi], f2[:, lo:hi], share_sb[:], back[:], ALU.mult, ALU.add)
             queue = nc.sync if k % 2 == 0 else nc.scalar
-            queue.dma_start(out=out[:, c : c + width], in_=result[:, c : c + width])
+            queue.dma_start(out=out[:, lo:hi], in_=result[:, lo:hi])

@@ -146,7 +146,14 @@ def tile_attend_quotaratio_lean_twiceput_heads_kernel(
         put(0, FIRST)
         nc.scalar.activation(root[:, FIRST:], s[:, FIRST:], ACT.Abs_reciprocal_sqrt)
         nc.scalar.activation(root_lam[:, FIRST:], root[:, FIRST:], ACT.Copy, scale=lam_sb[:])
-        put(FIRST, I)
+        nc.vector.tensor_tensor(
+            f1[:].indirect(entries(list1, FIRST, I)), root[:, FIRST:], root_lam[:, FIRST:], ALU.mult
+        )
+        square = sb.tile([P, I - FIRST], F32, name="square")
+        w = sb.tile([P, I - FIRST], F32, name="w")
+        nc.scalar.activation(square[:], root[:, FIRST:], ACT.Square)
+        nc.scalar.activation(w[:], square[:], ACT.Copy, scale=lam_sb[:])
+        nc.vector.tensor_copy(f2[:].indirect(entries(list4, FIRST, I)), w[:])
 
         old_sb = sb.tile([P, T], F32, name="old_sb")
         nc.sync.dma_start(out=old_sb[:], in_=old)

from contextlib import ExitStack

import concourse.mybir as mybir
from concourse.masks import make_identity

D, T, I, Q = 512, 1024, 512, 128
FLOPS = 2 * 2 * D * T * Q

F32 = mybir.dt.float32
BF16 = mybir.dt.bfloat16
I32 = mybir.dt.int32
U32 = mybir.dt.uint32
U16 = mybir.dt.uint16
U8 = mybir.dt.uint8
FP8X4 = mybir.dt.float8_e4m3fn_x4
ALU = mybir.AluOpType
ACT = mybir.ActivationFunctionType

P = 128
PACK = 4
BANK = 512
GROUP = 16
HALF = I // 2
FIRST = 128
STORES = 4


def tile_attend_quotaratio_lean_twiceput_heads_kernel(
    tc, query, query2, keys_words, keys_scales, lam, old, share2, offs, offs2, offs3, offs4, out
):
    nc = tc.nc
    with ExitStack() as ctx:
        sb = ctx.enter_context(tc.tile_pool(name="sb", bufs=1))
        ps = ctx.enter_context(tc.psum_pool(name="ps", bufs=1))

        def entries(list_tile, lo, hi):
            return list_tile[:, lo // GROUP : hi // GROUP]

        key_scales = sb.tile([P, T], U8, name="key_scales", align_bytes=64)
        nc.gpsimd.memset(key_scales[:].bitcast(I32), 0)

        raw = [sb.tile([P, PACK, Q], F32, name="raw%d" % n, tag="raw%d" % n) for n in range(2)]
        nc.sync.dma_start(out=raw[0][:], in_=query.rearrange("(p j) q -> p j q", j=PACK))
        scales_hbm = keys_scales[0].bitcast(I32)
        for quad in range(4):
            nc.sync.dma_start(
                out=key_scales[32 * quad : 32 * quad + 4, :].bitcast(I32),
                in_=scales_hbm[4 * quad : 4 * quad + 4, :],
            )
        nc.sync.dma_start(out=raw[1][:], in_=query2.rearrange("(p j) q -> p j q", j=PACK))
        words_hbm = keys_words[0].rearrange("p n t -> p (n t)").bitcast(I32)
        key_words = []
        for h in range(T // BANK):
            t = sb.tile([P, BANK], U32, name="key_words%d" % h, align_bytes=64)
            nc.sync.dma_start(out=t[:].bitcast(I32), in_=words_hbm[:, h * BANK : (h + 1) * BANK])
            key_words.append(t)
        lam_sb = sb.tile([P, 1], F32, name="lam_sb")
        nc.sync.dma_start(out=lam_sb[:], in_=lam)
        lists = []
        for n, src in enumerate((offs, offs2, offs3, offs4)):
            t = sb.tile([P, I // GROUP], U16, name="list%d" % n)
            nc.sync.dma_start(t[:], src)
            lists.append(t)
        list1, list2, list3, list4 = lists
        share_sb = sb.tile([P, 1], F32, name="share_sb")
        nc.sync.dma_start(out=share_sb[:], in_=share2)

        ident = sb.tile([P, P], F32, name="ident")
        make_identity(nc, ident[:])
        f1 = sb.tile([P, T], F32, name="f1")
        f2 = sb.tile([P, T], F32, name="f2")
        nc.vector.memset(f1[:], 0.0)
        nc.vector.memset(f2[:], 0.0)

        a = sb.tile([P, T], F32, name="a")
        b = sb.tile([P, T], F32, name="b")
        pieces = (
            ((0, 512, 0, nc.vector.tensor_copy), (512, 768, 1, nc.scalar.copy), (768, 1024, 2, nc.scalar.copy)),
            ((512, 1024, 3, nc.scalar.copy), (0, 512, 0, nc.scalar.copy)),
        )
        for n, scores in enumerate((a, b)):
            grouped = sb.tile([P, Q, PACK], BF16, name="grouped%d" % n, align_bytes=64)
            codes = sb.tile([P, Q], U32, name="codes%d" % n, align_bytes=64)
            scales = sb.tile([P, Q], U8, name="scales%d" % n, align_bytes=64)
            nc.vector.tensor_copy(
                out=grouped[:].rearrange("p (c i) t -> p c t i", i=4),
                in_=raw[n][:].rearrange("p t (c i) -> p c t i", i=4),
            )
            nc.vector.quantize_mx(
                out=codes[:].bitcast(FP8X4), scales=scales[:], in_=grouped[:].rearrange("p q t -> p (q t)")
            )
            for lo, hi, slot, copy in pieces[n]:
                bank = ps.tile([P, hi - lo], F32, name="score%d_%d" % (n, lo), tag="bank%d" % slot)
                nc.tensor.matmul_mx(
                    out=bank[:],
                    lhsT=codes[:].bitcast(FP8X4),
                    lhsT_scale=scales[:],
                    rhs=key_words[lo // BANK][:, lo % BANK : lo % BANK + hi - lo].bitcast(FP8X4),
                    rhs_scale=key_scales[:, lo:hi],
                    start=True,
                    stop=True,
                )
                copy(out=scores[:, lo:hi], in_=bank[:])

        a1 = sb.tile([P, I], F32, name="a1")
        nc.vector.tensor_copy(out=a1[:, :HALF], in_=a[:].indirect(entries(list1, 0, HALF)))
        nc.scalar.activation(a1[:, HALF:], a[:].indirect(entries(list1, HALF, I)), ACT.Copy)

        d2 = sb.tile([P, I], F32, name="d2")
        d3 = sb.tile([P, I], F32, name="d3")
        u = sb.tile([P, I], F32, name="u")
        v = sb.tile([P, I], F32, name="v")
        s = sb.tile([P, I], F32, name="s")

        def ratio(lo, window, list_tile, diff, power):
            cols = slice(lo, lo + HALF)
            nc.vector.tensor_tensor(
                diff[:, cols], window[:].indirect(entries(list_tile, lo, lo + HALF)), a1[:, cols], ALU.subtract
            )
            nc.scalar.activation(power[:, cols], diff[:, cols], ACT.Exp)

        def total(lo):
            cols = slice(lo, lo + HALF)
            nc.vector.scalar_tensor_tensor(s[:, cols], u[:, cols], 1.0, v[:, cols], ALU.add, ALU.add)

        root = sb.tile([P, I], F32, name="root")
        root_lam = sb.tile([P, I], F32, name="root_lam")

        def put(lo, hi):
            for window, list_tile in ((f1, list1), (f2, list4)):
                nc.vector.tensor_tensor(
                    window[:].indirect(entries(list_tile, lo, hi)), root[:, lo:hi], root_lam[:, lo:hi], ALU.mult
                )

        nc.scalar.copy(root_lam[:, :FIRST], lam_sb[:].to_broadcast([P, FIRST]))
        ratio(0, a, list2, d2, u)
        ratio(0, b, list3, d3, v)
        a2 = sb.tile([P, HALF], F32, name="a2")
        nc.scalar.activation(a2[:], a[:].indirect(entries(list2, HALF, I)), ACT.Copy)
        ratio(HALF, b, list3, d3, v)
        total(0)
        nc.vector.tensor_tensor(d2[:, HALF:], a2[:], a1[:, HALF:], ALU.subtract)
        nc.scalar.activation(u[:, HALF:], d2[:, HALF:], ACT.Exp)
        nc.vector.reciprocal(root[:, :FIRST], s[:, :FIRST])
        total(HALF)
        put(0, FIRST)
        nc.scalar.activation(root[:, FIRST:], s[:, FIRST:], ACT.Abs_reciprocal_sqrt)
        nc.scalar.activation(root_lam[:, FIRST:], root[:, FIRST:], ACT.Copy, scale=lam_sb[:])
        nc.vector.tensor_tensor(
            f1[:].indirect(entries(list1, FIRST, I)), root[:, FIRST:], root_lam[:, FIRST:], ALU.mult
        )
        square = sb.tile([P, I - FIRST], F32, name="square")
        w = sb.tile([P, I - FIRST], F32, name="w")
        nc.scalar.activation(square[:], root[:, FIRST:], ACT.Square)
        nc.scalar.activation(w[:], square[:], ACT.Copy, scale=lam_sb[:])
        nc.vector.tensor_copy(f2[:].indirect(entries(list4, FIRST, I)), w[:])

        old_sb = sb.tile([P, T], F32, name="old_sb")
        nc.sync.dma_start(out=old_sb[:], in_=old)
        spans = ((0, 256), (256, 512), (512, 896), (896, 1024))
        turned = []
        for k, (lo, hi) in enumerate(spans):
            bank = ps.tile([P, hi - lo], F32, name="turned%d" % k, tag="bank%d" % (4 + k))
            for c in range(lo, hi, P):
                nc.tensor.matmul(bank[:, c - lo : c - lo + P], lhsT=old_sb[:, c : c + P], rhs=ident[:],
                                 start=(c == lo), stop=False, is_transpose=True)
            turned.append(bank)
        for k, (lo, hi) in enumerate(spans):
            for c in range(lo, hi, P):
                nc.tensor.matmul(turned[k][:, c - lo : c - lo + P], lhsT=f1[:, c : c + P], rhs=ident[:],
                                 start=False, stop=(c + P == hi), is_transpose=True)
        result = sb.tile([P, T], F32, name="result")
        for k, (lo, hi) in enumerate(spans):
            staged = sb.tile([P, hi - lo], F32, name="staged%d" % k)
            nc.scalar.copy(out=staged[:], in_=turned[k][:])
            back = ps.tile([P, hi - lo], F32, name="back%d" % k, tag="bank%d" % k)
            for c in range(0, hi - lo, P):
                nc.tensor.transpose(back[:, c : c + P], staged[:, c : c + P], ident[:])
            nc.vector.scalar_tensor_tensor(result[:, lo:hi], f2[:, lo:hi], share_sb[:], back[:], ALU.mult, ALU.add)
            queue = nc.sync if k % 2 == 0 else nc.scalar
            queue.dma_start(out=out[:, lo:hi], in_=result[:, lo:hi])
